import numpy as np
import ml_dtypes


def mxq(x, axis, fmt="e4m3"):
    dtype, down = {"e4m3": (ml_dtypes.float8_e4m3fn, 7), "e5m2": (ml_dtypes.float8_e5m2, 14)}[fmt]
    v = np.moveaxis(np.asarray(x, np.float32).astype(ml_dtypes.bfloat16).astype(np.float64), axis, -1)
    blocks = v.reshape(v.shape[:-1] + (-1, 32))
    amax = np.abs(blocks).max(-1, keepdims=True)
    byte = np.maximum(np.where(amax > 0, np.frexp(amax)[1] - 1 + 127, 0) - down, 1)
    scale = np.exp2(byte - 127.0)
    codes = (blocks / scale).astype(np.float32).astype(dtype).astype(np.float64)
    return np.moveaxis((codes * scale).reshape(v.shape), -1, axis)


WIDE = False


def mx_kscale(k):
    if not WIDE:
        return np.ones(k)
    levels = np.array([30, -30])
    if k % 512:
        return np.exp2(np.random.permutation(np.resize(levels, k // 32))).repeat(32)
    a = np.empty((k // 512, 16))
    for p in range(k // 512):
        a[p, :8] = np.random.permutation(np.resize(levels, 8))
        for g in range(8):
            far = levels[np.abs(levels - a[p, g]) >= 10]
            a[p, g + 8] = far[np.random.randint(len(far))]
    return np.exp2(a.ravel()).repeat(32)


def f64(x):
    return np.asarray(x).astype(np.float64)


def striped(idx):
    return np.tile(np.asarray(idx).reshape(-1, 16).T, (8, 1)).astype(np.uint16)


def unstriped(offs):
    return offs[:16].T.reshape(-1).astype(np.int64)


E2M1 = np.array([0.0, 0.5, 1.0, 1.5, 2.0, 3.0, 4.0, 6.0, -0.0, -0.5, -1.0, -1.5, -2.0, -3.0, -4.0, -6.0])


def pack_weight(w, fmt):
    k, n = w.shape
    w = f64(np.asarray(w, np.float32).astype(ml_dtypes.bfloat16)).reshape(k // 32, 32, n)
    amax = np.abs(w).max(1)
    if fmt == "e4m3":
        byte = np.frexp(amax)[1] - 1 + 127 - 7
    else:
        mant, ex = np.frexp(amax / 6.0)
        byte = np.where(mant > 0.5, ex, ex - 1) + 127
    byte = np.clip(np.where(amax > 0, byte, 1), 1, 254)
    scaled = (w * np.exp2(127.0 - byte)[:, None, :]).reshape(k, n).astype(np.float32)
    by_word = np.ascontiguousarray(scaled.reshape(k // 512, 128, 4, n).transpose(0, 1, 3, 2))
    if fmt == "e4m3":
        words = by_word.astype(ml_dtypes.float8_e4m3fn).view(np.uint8)
    else:
        c = by_word.astype(ml_dtypes.float4_e2m1fn).view(np.uint8) & 0xF
        words = (c[..., 0::2] | (c[..., 1::2] << 4)).reshape(k // 512, 128, 2 * n)
    return np.ascontiguousarray(words), np.ascontiguousarray(byte.astype(np.uint8).reshape(k // 512, 16, n))


def unpack_weight(words, scales, fmt):
    g, _, n = scales.shape
    words = np.ascontiguousarray(words).reshape(g, 128, n, -1)
    if fmt == "e4m3":
        vals = words.view(ml_dtypes.float8_e4m3fn).astype(np.float64)
    else:
        nib = np.empty((g, 128, n, 4), np.uint8)
        nib[..., 0::2] = words & 0xF
        nib[..., 1::2] = words >> 4
        vals = E2M1[nib]
    vals = vals * np.repeat(np.exp2(scales.astype(np.float64) - 127.0), 8, axis=1)[..., None]
    return vals.transpose(0, 1, 3, 2).reshape(g * 512, n)


def bf(x):
    return np.asarray(x, np.float32).astype(ml_dtypes.bfloat16)


def planes(Y):
    r, m = Y.shape
    b = f64(bf(Y)).reshape(r // 32, 32, m)
    amax = np.abs(b).max(1)
    byte = np.clip(np.where(amax > 0, np.frexp(amax)[1] - 1 + 127 - 7, 1), 1, 254)
    codes = (b * np.exp2(127.0 - byte)[:, None, :]).reshape(r, m).astype(np.float32).astype(ml_dtypes.float8_e4m3fn).view(np.uint8)
    words = codes.reshape(r // 512, 128, 4, m).transpose(0, 1, 3, 2)
    return np.ascontiguousarray(words), np.ascontiguousarray(byte.astype(np.uint8).reshape(r // 512, 16, m))


K, N, T, J = 512, 512, 2048, 512


def setup_inputs():
    n = np.random.standard_normal
    idx = np.random.permutation(T)[:J]
    fk = mx_kscale(K)
    fn = mx_kscale(N)
    xtp = pack_weight(n((K, T)) / fk[:, None], "e2m1")
    wp = pack_weight(n((K, N)) * 1 / np.sqrt(K) * fk[:, None], "e4m3")
    wtp = pack_weight(n((N, K)) * 1 / np.sqrt(N) / fn[:, None], "e2m1")
    return {
        "xt_words": xtp[0],
        "xt_scales": xtp[1],
        "w_words": wp[0],
        "w_scales": wp[1],
        "tea": (np.random.uniform(-0.9, 0.9, (N, T))).astype(np.float32),
        "us": (np.random.uniform(0.5, 2.0, (N, 1)) * fn[:, None]).astype(np.float32),
        "wt_words": wtp[0],
        "wt_scales": wtp[1],
        "res": (0.3 * n((K, J))).astype(np.float32),
        "offs": striped(idx),
    }


def reference(xt_words, xt_scales, w_words, w_scales, tea, us, wt_words, wt_scales, res, offs):
    idx = unstriped(offs)
    xtu = unpack_weight(xt_words, xt_scales, "e2m1")
    wu = unpack_weight(w_words, w_scales, "e4m3")
    wtu = unpack_weight(wt_words, wt_scales, "e2m1")
    xtidxg = xtu[:, idx]
    z = wu.T @ xtidxg
    d = (np.tanh(z) - f64(tea)[:, idx]) * f64(us)
    dq = mxq(d, 0, "e5m2")
    dx = wtu.T @ dq
    y = dx + f64(res)
    words, scales = planes(y)
    return y, words, scales

@@ -1,0 +1,167 @@
+from contextlib import ExitStack
+
+import concourse.mybir as mybir
+
+F32 = mybir.dt.float32
+BF16 = mybir.dt.bfloat16
+I32 = mybir.dt.int32
+U32 = mybir.dt.uint32
+U16 = mybir.dt.uint16
+U8 = mybir.dt.uint8
+E4M3X4 = mybir.dt.float8_e4m3fn_x4
+E5M2X4 = mybir.dt.float8_e5m2_x4
+E2M1X4 = mybir.dt.float4_e2m1fn_x4
+ACT = mybir.ActivationFunctionType
+ALU = mybir.AluOpType
+
+P = 128
+PACK = 4
+K, N, T, J = 512, 512, 2048, 512
+HALF = J // 2
+
+FLOPS = 2 * K * N * J + 2 * N * K * J
+
+
+def load_scale_rows(nc, plane, scales):
+    for q in range(4):
+        nc.sync.dma_start(out=plane[32 * q : 32 * q + 4, :].bitcast(I32), in_=scales[0, 4 * q : 4 * q + 4, :].bitcast(I32))
+
+
+def tile_list_feature_match_back_pl_kernel(
+    tc, xt_words, xt_scales, w_words, w_scales, tea, us, wt_words, wt_scales, res, offs, out_0, out_1, out_2
+):
+    nc = tc.nc
+    with ExitStack() as ctx:
+        sb = ctx.enter_context(tc.tile_pool(name="sb", bufs=1))
+        ps = ctx.enter_context(tc.psum_pool(name="ps", bufs=1))
+
+        offsets = sb.tile([P, J // 16], U16, name="offsets")
+        x_words = sb.tile([P, T], U16, name="x_words", align_bytes=64)
+        x_plane = sb.tile([P, T], U8, name="x_plane", align_bytes=64)
+        w_raw = sb.tile([P, N], I32, name="w_raw", align_bytes=64)
+        w_plane = sb.tile([P, N], U8, name="w_plane", align_bytes=64)
+        wt_raw = sb.tile([P, 2 * K], U8, name="wt_raw", align_bytes=64)
+        wt_plane = sb.tile([P, K], U8, name="wt_plane", align_bytes=64)
+        us_sb = sb.tile([P, PACK], F32, name="us_sb")
+        tea_sb = [sb.tile([P, T], F32, name=f"tea{t}", align_bytes=64) for t in range(PACK)]
+        res_sb = sb.tile([P, PACK, J], F32, name="res_sb", align_bytes=64)
+
+        for plane in (x_plane, w_plane, wt_plane):
+            nc.vector.memset(plane[:].bitcast(I32), 0)
+
+        tea_rows = tea.rearrange("(p t) c -> t p c", t=PACK)
+        nc.sync.dma_start(offsets[:], offs)
+        nc.sync.dma_start(out=x_words[:].bitcast(I32), in_=xt_words[0].bitcast(I32))
+        load_scale_rows(nc, x_plane, xt_scales)
+        nc.sync.dma_start(out=w_raw[:], in_=w_words[0].rearrange("p n t -> p (n t)").bitcast(I32))
+        nc.sync.dma_start(out=tea_sb[0][:], in_=tea_rows[0])
+        load_scale_rows(nc, w_plane, w_scales)
+        nc.sync.dma_start(out=wt_raw[:].bitcast(I32), in_=wt_words[0].bitcast(I32))
+        nc.sync.dma_start(out=us_sb[:], in_=us.rearrange("(p t) o -> p (t o)", t=PACK))
+        nc.sync.dma_start(out=tea_sb[1][:], in_=tea_rows[1])
+        load_scale_rows(nc, wt_plane, wt_scales)
+        nc.sync.dma_start(out=tea_sb[2][:], in_=tea_rows[2])
+        nc.sync.dma_start(out=tea_sb[3][:], in_=tea_rows[3])
+        nc.sync.dma_start(out=res_sb[:], in_=res.rearrange("(p t) j -> p t j", t=PACK))
+
+        xg_words = sb.tile([P, J], U16, name="xg_words", align_bytes=64)
+        xg_plane = sb.tile([P, J], U8, name="xg_plane", align_bytes=64)
+        nc.vector.tensor_copy(xg_words[:], x_words[:].indirect(offsets[:]))
+        nc.vector.tensor_copy(xg_plane[:], x_plane[:].indirect(offsets[:]))
+
+        w_dealt = sb.tile([P, N], I32, name="w_dealt", align_bytes=64)
+        w_plane_dealt = sb.tile([P, N], U8, name="w_plane_dealt", align_bytes=64)
+        nc.vector.tensor_copy(
+            out=w_dealt[:].rearrange("p (t m) -> p t m", t=PACK), in_=w_raw[:].rearrange("p (m t) -> p t m", t=PACK)
+        )
+        nc.vector.tensor_copy(
+            out=w_plane_dealt[:].rearrange("p (t m) -> p t m", t=PACK),
+            in_=w_plane[:].rearrange("p (m t) -> p t m", t=PACK),
+        )
+
+        tanh_z = []
+        for t in range(PACK):
+            cols = slice(P * t, P * (t + 1))
+            z = ps.tile([P, J], F32, name=f"z{t}")
+            nc.tensor.matmul_mx(
+                out=z[:],
+                lhsT=w_dealt[:, cols].bitcast(E4M3X4),
+                lhsT_scale=w_plane_dealt[:, cols],
+                rhs=xg_words[:].bitcast(E2M1X4),
+                rhs_scale=xg_plane[:],
+                start=True,
+                stop=True,
+            )
+            th = sb.tile([P, J], F32, name=f"tanh{t}", align_bytes=64)
+            nc.scalar.activation(out=th[:], in_=z[:], func=ACT.Tanh)
+            tanh_z.append(th)
+
+        neg_us = sb.tile([P, PACK], F32, name="neg_us")
+        nc.vector.tensor_scalar(out=neg_us[:], in0=us_sb[:], scalar1=-1.0, scalar2=None, op0=ALU.mult)
+
+        wt_dealt = sb.tile([P, 2 * K], U8, name="wt_dealt", align_bytes=64)
+        wt_plane_dealt = sb.tile([P, K], U8, name="wt_plane_dealt", align_bytes=64)
+        nc.vector.tensor_copy(
+            out=wt_dealt[:].bitcast(U16).rearrange("p (t m) -> p t m", t=PACK),
+            in_=wt_raw[:].bitcast(U16).rearrange("p (m t) -> p t m", t=PACK),
+        )
+        nc.vector.tensor_copy(
+            out=wt_plane_dealt[:].rearrange("p (t m) -> p t m", t=PACK),
+            in_=wt_plane[:].rearrange("p (m t) -> p t m", t=PACK),
+        )
+
+        d_bf = [sb.tile([P, HALF, PACK], BF16, name=f"d_bf{h}", align_bytes=64) for h in range(2)]
+        d_words = sb.tile([P, J], U32, name="d_words", align_bytes=64)
+        d_plane = sb.tile([P, J], U8, name="d_plane", align_bytes=64)
+        for t in range(PACK):
+            for h in range(2):
+                diff = sb.tile([P, HALF], F32, name=f"diff{t}_{h}", align_bytes=64)
+                nc.vector.tensor_tensor(
+                    diff[:],
+                    tea_sb[t][:].indirect(offsets[:, h * HALF // 16 : (h + 1) * HALF // 16]),
+                    tanh_z[t][:, h * HALF : (h + 1) * HALF],
+                    ALU.subtract,
+                )
+                if t < 2 or h == 0:
+                    nc.scalar.activation(out=d_bf[h][:, :, t], in_=diff[:], func=ACT.Copy, scale=neg_us[:, t : t + 1])
+                else:
+                    nc.vector.tensor_scalar(
+                        out=d_bf[h][:, :, t], in0=diff[:], scalar1=neg_us[:, t : t + 1], scalar2=None, op0=ALU.mult
+                    )
+        for h in range(2):
+            cols = slice(h * HALF, (h + 1) * HALF)
+            nc.vector.quantize_mx(
+                out=d_words[:, cols].bitcast(E5M2X4),
+                scales=d_plane[:, cols],
+                in_=d_bf[h][:].rearrange("p j t -> p (j t)"),
+            )
+
+        y = [sb.tile([P, 2, J], F32, name=f"y{u}", align_bytes=64) for u in range(2)]
+        out_rows = out_0.rearrange("(p t) j -> t p j", t=PACK)
+        for t in range(PACK):
+            dx = ps.tile([P, J], F32, name=f"dx{t}")
+            nc.tensor.matmul_mx(
+                out=dx[:],
+                lhsT=wt_dealt[:, 2 * P * t : 2 * P * (t + 1)].bitcast(E2M1X4),
+                lhsT_scale=wt_plane_dealt[:, P * t : P * (t + 1)],
+                rhs=d_words[:].bitcast(E5M2X4),
+                rhs_scale=d_plane[:],
+                start=True,
+                stop=True,
+            )
+            nc.vector.tensor_tensor(y[t // 2][:, t % 2, :], dx[:], res_sb[:, t, :], ALU.add)
+            nc.sync.dma_start(out=out_rows[t], in_=y[t // 2][:, t % 2, :])
+
+        y_bf = sb.tile([P, J, PACK], BF16, name="y_bf", align_bytes=64)
+        nc.scalar.copy(out=y_bf[:, :, 0:2], in_=y[0][:].rearrange("p e j -> p j e"))
+        nc.vector.tensor_copy(out=y_bf[:, :, 2:4], in_=y[1][:].rearrange("p e j -> p j e"))
+        y_words = sb.tile([P, J], U32, name="y_words", align_bytes=64)
+        y_plane = sb.tile([P, J], U8, name="y_plane", align_bytes=64)
+        nc.vector.quantize_mx(
+            out=y_words[:].bitcast(E4M3X4), scales=y_plane[:], in_=y_bf[:].rearrange("p j t -> p (j t)")
+        )
+        nc.sync.dma_start(out=out_1[0].rearrange("p j t -> p (j t)").bitcast(I32), in_=y_words[:].bitcast(I32))
+        for q in range(4):
+            nc.scalar.dma_start(
+                out=out_2[0, 4 * q : 4 * q + 4, :].bitcast(I32), in_=y_plane[32 * q : 32 * q + 4, :].bitcast(I32)
+            )

@@ -18,19 +18,21 @@ P = 128
 PACK = 4
 K, N, T, J = 512, 512, 2048, 512
 HALF = J // 2
+HEAD = T // 4
 
 FLOPS = 2 * K * N * J + 2 * N * K * J
 
 
-def load_scale_rows(nc, plane, scales):
+def load_scale_rows(queue, plane, scales):
     for q in range(4):
-        nc.sync.dma_start(out=plane[32 * q : 32 * q + 4, :].bitcast(I32), in_=scales[0, 4 * q : 4 * q + 4, :].bitcast(I32))
+        queue.dma_start(out=plane[32 * q : 32 * q + 4, :].bitcast(I32), in_=scales[0, 4 * q : 4 * q + 4, :].bitcast(I32))
 
 
 def tile_list_feature_match_back_pl_kernel(
     tc, xt_words, xt_scales, w_words, w_scales, tea, us, wt_words, wt_scales, res, offs, out_0, out_1, out_2
 ):
     nc = tc.nc
+    halves = (slice(0, HALF), slice(HALF, J))
     with ExitStack() as ctx:
         sb = ctx.enter_context(tc.tile_pool(name="sb", bufs=1))
         ps = ctx.enter_context(tc.psum_pool(name="ps", bufs=1))
@@ -46,20 +48,22 @@ def tile_list_feature_match_back_pl_kernel(
         tea_sb = [sb.tile([P, T], F32, name=f"tea{t}", align_bytes=64) for t in range(PACK)]
         res_sb = sb.tile([P, PACK, J], F32, name="res_sb", align_bytes=64)
 
-        for plane in (x_plane, w_plane, wt_plane):
-            nc.vector.memset(plane[:].bitcast(I32), 0)
+        nc.vector.memset(x_plane[:].bitcast(I32), 0)
+        nc.vector.memset(w_plane[:].bitcast(I32), 0)
+        nc.vector.memset(wt_plane[:].bitcast(I32), 0)
 
         tea_rows = tea.rearrange("(p t) c -> t p c", t=PACK)
         nc.sync.dma_start(offsets[:], offs)
         nc.sync.dma_start(out=x_words[:].bitcast(I32), in_=xt_words[0].bitcast(I32))
-        load_scale_rows(nc, x_plane, xt_scales)
+        load_scale_rows(nc.sync, x_plane, xt_scales)
         nc.sync.dma_start(out=w_raw[:], in_=w_words[0].rearrange("p n t -> p (n t)").bitcast(I32))
-        nc.sync.dma_start(out=tea_sb[0][:], in_=tea_rows[0])
-        load_scale_rows(nc, w_plane, w_scales)
-        nc.sync.dma_start(out=wt_raw[:].bitcast(I32), in_=wt_words[0].bitcast(I32))
+        nc.sync.dma_start(out=tea_sb[0][:, :HEAD], in_=tea_rows[0][:, :HEAD])
+        load_scale_rows(nc.sync, w_plane, w_scales)
+        nc.sync.dma_start(out=tea_sb[0][:, HEAD:], in_=tea_rows[0][:, HEAD:])
         nc.sync.dma_start(out=us_sb[:], in_=us.rearrange("(p t) o -> p (t o)", t=PACK))
         nc.sync.dma_start(out=tea_sb[1][:], in_=tea_rows[1])
-        load_scale_rows(nc, wt_plane, wt_scales)
+        nc.sync.dma_start(out=wt_raw[:].bitcast(I32), in_=wt_words[0].bitcast(I32))
+        load_scale_rows(nc.sync, wt_plane, wt_scales)
         nc.sync.dma_start(out=tea_sb[2][:], in_=tea_rows[2])
         nc.sync.dma_start(out=tea_sb[3][:], in_=tea_rows[3])
         nc.sync.dma_start(out=res_sb[:], in_=res.rearrange("(p t) j -> p t j", t=PACK))
@@ -96,9 +100,6 @@ def tile_list_feature_match_back_pl_kernel(
             nc.scalar.activation(out=th[:], in_=z[:], func=ACT.Tanh)
             tanh_z.append(th)
 
-        neg_us = sb.tile([P, PACK], F32, name="neg_us")
-        nc.vector.tensor_scalar(out=neg_us[:], in0=us_sb[:], scalar1=-1.0, scalar2=None, op0=ALU.mult)
-
         wt_dealt = sb.tile([P, 2 * K], U8, name="wt_dealt", align_bytes=64)
         wt_plane_dealt = sb.tile([P, K], U8, name="wt_plane_dealt", align_bytes=64)
         nc.vector.tensor_copy(
@@ -123,10 +124,10 @@ def tile_list_feature_match_back_pl_kernel(
                     ALU.subtract,
                 )
                 if t < 2 or h == 0:
-                    nc.scalar.activation(out=d_bf[h][:, :, t], in_=diff[:], func=ACT.Copy, scale=neg_us[:, t : t + 1])
+                    nc.scalar.activation(out=d_bf[h][:, :, t], in_=diff[:], func=ACT.Copy, scale=us_sb[:, t : t + 1])
                 else:
                     nc.vector.tensor_scalar(
-                        out=d_bf[h][:, :, t], in0=diff[:], scalar1=neg_us[:, t : t + 1], scalar2=None, op0=ALU.mult
+                        out=d_bf[h][:, :, t], in0=diff[:], scalar1=us_sb[:, t : t + 1], scalar2=None, op0=ALU.mult
                     )
         for h in range(2):
             cols = slice(h * HALF, (h + 1) * HALF)
@@ -149,19 +150,28 @@ def tile_list_feature_match_back_pl_kernel(
                 start=True,
                 stop=True,
             )
-            nc.vector.tensor_tensor(y[t // 2][:, t % 2, :], dx[:], res_sb[:, t, :], ALU.add)
+            pieces = (slice(0, J),) if t < PACK - 1 else halves
+            for cols in pieces:
+                nc.vector.tensor_tensor(y[t // 2][:, t % 2, cols], res_sb[:, t, cols], dx[:, cols], ALU.subtract)
             nc.sync.dma_start(out=out_rows[t], in_=y[t // 2][:, t % 2, :])
 
-        y_bf = sb.tile([P, J, PACK], BF16, name="y_bf", align_bytes=64)
-        nc.scalar.copy(out=y_bf[:, :, 0:2], in_=y[0][:].rearrange("p e j -> p j e"))
-        nc.vector.tensor_copy(out=y_bf[:, :, 2:4], in_=y[1][:].rearrange("p e j -> p j e"))
+        y_bf = [sb.tile([P, HALF, PACK], BF16, name=f"y_bf{h}", align_bytes=64) for h in range(2)]
+        for h, cols in enumerate(halves):
+            nc.scalar.copy(out=y_bf[h][:, :, 0:2], in_=y[0][:, :, cols].rearrange("p e j -> p j e"))
+        for h, cols in enumerate(halves):
+            nc.vector.tensor_copy(out=y_bf[h][:, :, 2:4], in_=y[1][:, :, cols].rearrange("p e j -> p j e"))
         y_words = sb.tile([P, J], U32, name="y_words", align_bytes=64)
         y_plane = sb.tile([P, J], U8, name="y_plane", align_bytes=64)
-        nc.vector.quantize_mx(
-            out=y_words[:].bitcast(E4M3X4), scales=y_plane[:], in_=y_bf[:].rearrange("p j t -> p (j t)")
-        )
-        nc.sync.dma_start(out=out_1[0].rearrange("p j t -> p (j t)").bitcast(I32), in_=y_words[:].bitcast(I32))
+        out_words = out_1[0].rearrange("p j t -> p (j t)").bitcast(I32)
+        for h, cols in enumerate(halves):
+            nc.vector.quantize_mx(
+                out=y_words[:, cols].bitcast(E4M3X4),
+                scales=y_plane[:, cols],
+                in_=y_bf[h][:].rearrange("p j t -> p (j t)"),
+            )
+            nc.sync.dma_start(out=out_words[:, cols], in_=y_words[:, cols].bitcast(I32))
         for q in range(4):
-            nc.scalar.dma_start(
+            queue = nc.scalar if q < 3 else nc.sync
+            queue.dma_start(
                 out=out_2[0, 4 * q : 4 * q + 4, :].bitcast(I32), in_=y_plane[32 * q : 32 * q + 4, :].bitcast(I32)
             )

@@ -18,14 +18,13 @@ P = 128
 PACK = 4
 K, N, T, J = 512, 512, 2048, 512
 HALF = J // 2
-HEAD = T // 4
 
 FLOPS = 2 * K * N * J + 2 * N * K * J
 
 
 def load_scale_rows(queue, plane, scales):
-    for q in range(4):
-        queue.dma_start(out=plane[32 * q : 32 * q + 4, :].bitcast(I32), in_=scales[0, 4 * q : 4 * q + 4, :].bitcast(I32))
+    for r in range(4):
+        queue.dma_start(out=plane[r:P:32, :].bitcast(I32), in_=scales[0, r:16:4, :].bitcast(I32))
 
 
 def tile_list_feature_match_back_pl_kernel(
@@ -41,7 +40,7 @@ def tile_list_feature_match_back_pl_kernel(
         x_words = sb.tile([P, T], U16, name="x_words", align_bytes=64)
         x_plane = sb.tile([P, T], U8, name="x_plane", align_bytes=64)
         w_raw = sb.tile([P, N], I32, name="w_raw", align_bytes=64)
-        w_plane = sb.tile([P, N], U8, name="w_plane", align_bytes=64)
+        w_plane = sb.tile([P, N], U8, name="w_plane", tag="w_plane_then_tea0", align_bytes=64)
         wt_raw = sb.tile([P, 2 * K], U8, name="wt_raw", align_bytes=64)
         wt_plane = sb.tile([P, K], U8, name="wt_plane", align_bytes=64)
         us_sb = sb.tile([P, PACK], F32, name="us_sb")
@@ -53,16 +52,15 @@ def tile_list_feature_match_back_pl_kernel(
         nc.vector.memset(wt_plane[:].bitcast(I32), 0)
 
         tea_rows = tea.rearrange("(p t) c -> t p c", t=PACK)
-        nc.sync.dma_start(offsets[:], offs)
         nc.sync.dma_start(out=x_words[:].bitcast(I32), in_=xt_words[0].bitcast(I32))
+        nc.sync.dma_start(offsets[:], offs)
         load_scale_rows(nc.sync, x_plane, xt_scales)
         nc.sync.dma_start(out=w_raw[:], in_=w_words[0].rearrange("p n t -> p (n t)").bitcast(I32))
-        nc.sync.dma_start(out=tea_sb[0][:, :HEAD], in_=tea_rows[0][:, :HEAD])
+        nc.sync.dma_start(out=tea_sb[0][:], in_=tea_rows[0])
         load_scale_rows(nc.sync, w_plane, w_scales)
-        nc.sync.dma_start(out=tea_sb[0][:, HEAD:], in_=tea_rows[0][:, HEAD:])
+        nc.sync.dma_start(out=wt_raw[:].bitcast(I32), in_=wt_words[0].bitcast(I32))
         nc.sync.dma_start(out=us_sb[:], in_=us.rearrange("(p t) o -> p (t o)", t=PACK))
         nc.sync.dma_start(out=tea_sb[1][:], in_=tea_rows[1])
-        nc.sync.dma_start(out=wt_raw[:].bitcast(I32), in_=wt_words[0].bitcast(I32))
         load_scale_rows(nc.sync, wt_plane, wt_scales)
         nc.sync.dma_start(out=tea_sb[2][:], in_=tea_rows[2])
         nc.sync.dma_start(out=tea_sb[3][:], in_=tea_rows[3])
@@ -82,6 +80,9 @@ def tile_list_feature_match_back_pl_kernel(
             out=w_plane_dealt[:].rearrange("p (t m) -> p t m", t=PACK),
             in_=w_plane[:].rearrange("p (m t) -> p t m", t=PACK),
         )
+
+        tea0_listed = sb.tile([P, J], F32, name="tea0_listed", tag="w_plane_then_tea0", align_bytes=64)
+        nc.vector.tensor_copy(tea0_listed[:], tea_sb[0][:].indirect(offsets[:]))
 
         tanh_z = []
         for t in range(PACK):
@@ -114,16 +115,24 @@ def tile_list_feature_match_back_pl_kernel(
         d_bf = [sb.tile([P, HALF, PACK], BF16, name=f"d_bf{h}", align_bytes=64) for h in range(2)]
         d_words = sb.tile([P, J], U32, name="d_words", align_bytes=64)
         d_plane = sb.tile([P, J], U8, name="d_plane", align_bytes=64)
-        for t in range(PACK):
-            for h in range(2):
+        diff01 = sb.tile([P, 2, J], F32, name="diff01", align_bytes=64)
+        d01 = sb.tile([P, 2, J], BF16, name="d01", align_bytes=64)
+        nc.vector.tensor_tensor(diff01[:, 0, :], tea0_listed[:], tanh_z[0][:], ALU.subtract)
+        nc.vector.tensor_tensor(diff01[:, 1, :], tea_sb[1][:].indirect(offsets[:]), tanh_z[1][:], ALU.subtract)
+        for t in range(2):
+            nc.scalar.activation(out=d01[:, t, :], in_=diff01[:, t, :], func=ACT.Copy, scale=us_sb[:, t : t + 1])
+        for h, cols in enumerate(halves):
+            nc.scalar.copy(out=d_bf[h][:, :, 0:2], in_=d01[:, :, cols].rearrange("p e j -> p j e"))
+        for t in range(2, PACK):
+            for h, cols in enumerate(halves):
                 diff = sb.tile([P, HALF], F32, name=f"diff{t}_{h}", align_bytes=64)
                 nc.vector.tensor_tensor(
                     diff[:],
                     tea_sb[t][:].indirect(offsets[:, h * HALF // 16 : (h + 1) * HALF // 16]),
-                    tanh_z[t][:, h * HALF : (h + 1) * HALF],
+                    tanh_z[t][:, cols],
                     ALU.subtract,
                 )
-                if t < 2 or h == 0:
+                if h == 0:
                     nc.scalar.activation(out=d_bf[h][:, :, t], in_=diff[:], func=ACT.Copy, scale=us_sb[:, t : t + 1])
                 else:
                     nc.vector.tensor_scalar(
@@ -170,8 +179,6 @@ def tile_list_feature_match_back_pl_kernel(
                 in_=y_bf[h][:].rearrange("p j t -> p (j t)"),
             )
             nc.sync.dma_start(out=out_words[:, cols], in_=y_words[:, cols].bitcast(I32))
-        for q in range(4):
-            queue = nc.scalar if q < 3 else nc.sync
-            queue.dma_start(
-                out=out_2[0, 4 * q : 4 * q + 4, :].bitcast(I32), in_=y_plane[32 * q : 32 * q + 4, :].bitcast(I32)
-            )
+        for r in range(4):
+            queue = nc.scalar if r < 2 else nc.sync
+            queue.dma_start(out=out_2[0, r:16:4, :].bitcast(I32), in_=y_plane[r:P:32, :].bitcast(I32))

from contextlib import ExitStack

import concourse.mybir as mybir

F32 = mybir.dt.float32
BF16 = mybir.dt.bfloat16
I32 = mybir.dt.int32
U32 = mybir.dt.uint32
U16 = mybir.dt.uint16
U8 = mybir.dt.uint8
E4M3X4 = mybir.dt.float8_e4m3fn_x4
E5M2X4 = mybir.dt.float8_e5m2_x4
E2M1X4 = mybir.dt.float4_e2m1fn_x4
ACT = mybir.ActivationFunctionType
ALU = mybir.AluOpType

P = 128
PACK = 4
K, N, T, J = 512, 512, 2048, 512
HALF = J // 2

FLOPS = 2 * K * N * J + 2 * N * K * J


def load_scale_rows(queue, plane, scales):
    for r in range(4):
        queue.dma_start(out=plane[r:P:32, :].bitcast(I32), in_=scales[0, r:16:4, :].bitcast(I32))


def tile_list_feature_match_back_pl_kernel(
    tc, xt_words, xt_scales, w_words, w_scales, tea, us, wt_words, wt_scales, res, offs, out_0, out_1, out_2
):
    nc = tc.nc
    halves = (slice(0, HALF), slice(HALF, J))
    with ExitStack() as ctx:
        sb = ctx.enter_context(tc.tile_pool(name="sb", bufs=1))
        ps = ctx.enter_context(tc.psum_pool(name="ps", bufs=1))

        offsets = sb.tile([P, J // 16], U16, name="offsets")
        x_words = sb.tile([P, T], U16, name="x_words", align_bytes=64)
        x_plane = sb.tile([P, T], U8, name="x_plane", align_bytes=64)
        w_raw = sb.tile([P, N], I32, name="w_raw", align_bytes=64)
        w_plane = sb.tile([P, N], U8, name="w_plane", tag="w_plane_then_tea0", align_bytes=64)
        wt_raw = sb.tile([P, 2 * K], U8, name="wt_raw", align_bytes=64)
        wt_plane = sb.tile([P, K], U8, name="wt_plane", align_bytes=64)
        us_sb = sb.tile([P, PACK], F32, name="us_sb")
        tea_sb = [sb.tile([P, T], F32, name=f"tea{t}", align_bytes=64) for t in range(PACK)]
        res_sb = sb.tile([P, PACK, J], F32, name="res_sb", align_bytes=64)

        nc.vector.memset(x_plane[:].bitcast(I32), 0)
        nc.vector.memset(w_plane[:].bitcast(I32), 0)
        nc.vector.memset(wt_plane[:].bitcast(I32), 0)

        tea_rows = tea.rearrange("(p t) c -> t p c", t=PACK)
        nc.sync.dma_start(out=x_words[:].bitcast(I32), in_=xt_words[0].bitcast(I32))
        nc.sync.dma_start(offsets[:], offs)
        load_scale_rows(nc.sync, x_plane, xt_scales)
        nc.sync.dma_start(out=w_raw[:], in_=w_words[0].rearrange("p n t -> p (n t)").bitcast(I32))
        nc.sync.dma_start(out=tea_sb[0][:], in_=tea_rows[0])
        load_scale_rows(nc.sync, w_plane, w_scales)
        nc.sync.dma_start(out=wt_raw[:].bitcast(I32), in_=wt_words[0].bitcast(I32))
        nc.sync.dma_start(out=us_sb[:], in_=us.rearrange("(p t) o -> p (t o)", t=PACK))
        nc.sync.dma_start(out=tea_sb[1][:], in_=tea_rows[1])
        load_scale_rows(nc.sync, wt_plane, wt_scales)
        nc.sync.dma_start(out=tea_sb[2][:], in_=tea_rows[2])
        nc.sync.dma_start(out=tea_sb[3][:], in_=tea_rows[3])
        nc.sync.dma_start(out=res_sb[:], in_=res.rearrange("(p t) j -> p t j", t=PACK))

        xg_words = sb.tile([P, J], U16, name="xg_words", align_bytes=64)
        xg_plane = sb.tile([P, J], U8, name="xg_plane", align_bytes=64)
        nc.vector.tensor_copy(xg_words[:], x_words[:].indirect(offsets[:]))
        nc.vector.tensor_copy(xg_plane[:], x_plane[:].indirect(offsets[:]))

        w_dealt = sb.tile([P, N], I32, name="w_dealt", align_bytes=64)
        w_plane_dealt = sb.tile([P, N], U8, name="w_plane_dealt", align_bytes=64)
        nc.vector.tensor_copy(
            out=w_dealt[:].rearrange("p (t m) -> p t m", t=PACK), in_=w_raw[:].rearrange("p (m t) -> p t m", t=PACK)
        )
        nc.vector.tensor_copy(
            out=w_plane_dealt[:].rearrange("p (t m) -> p t m", t=PACK),
            in_=w_plane[:].rearrange("p (m t) -> p t m", t=PACK),
        )

        tea0_listed = sb.tile([P, J], F32, name="tea0_listed", tag="w_plane_then_tea0", align_bytes=64)
        nc.vector.tensor_copy(tea0_listed[:], tea_sb[0][:].indirect(offsets[:]))

        tanh_z = []
        for t in range(PACK):
            cols = slice(P * t, P * (t + 1))
            z = ps.tile([P, J], F32, name=f"z{t}")
            nc.tensor.matmul_mx(
                out=z[:],
                lhsT=w_dealt[:, cols].bitcast(E4M3X4),
                lhsT_scale=w_plane_dealt[:, cols],
                rhs=xg_words[:].bitcast(E2M1X4),
                rhs_scale=xg_plane[:],
                start=True,
                stop=True,
            )
            th = sb.tile([P, J], F32, name=f"tanh{t}", align_bytes=64)
            nc.scalar.activation(out=th[:], in_=z[:], func=ACT.Tanh)
            tanh_z.append(th)

        wt_dealt = sb.tile([P, 2 * K], U8, name="wt_dealt", align_bytes=64)
        wt_plane_dealt = sb.tile([P, K], U8, name="wt_plane_dealt", align_bytes=64)
        nc.vector.tensor_copy(
            out=wt_dealt[:].bitcast(U16).rearrange("p (t m) -> p t m", t=PACK),
            in_=wt_raw[:].bitcast(U16).rearrange("p (m t) -> p t m", t=PACK),
        )
        nc.vector.tensor_copy(
            out=wt_plane_dealt[:].rearrange("p (t m) -> p t m", t=PACK),
            in_=wt_plane[:].rearrange("p (m t) -> p t m", t=PACK),
        )

        d_bf = [sb.tile([P, HALF, PACK], BF16, name=f"d_bf{h}", align_bytes=64) for h in range(2)]
        d_words = sb.tile([P, J], U32, name="d_words", align_bytes=64)
        d_plane = sb.tile([P, J], U8, name="d_plane", align_bytes=64)
        diff01 = sb.tile([P, 2, J], F32, name="diff01", align_bytes=64)
        d01 = sb.tile([P, 2, J], BF16, name="d01", align_bytes=64)
        nc.vector.tensor_tensor(diff01[:, 0, :], tea0_listed[:], tanh_z[0][:], ALU.subtract)
        nc.vector.tensor_tensor(diff01[:, 1, :], tea_sb[1][:].indirect(offsets[:]), tanh_z[1][:], ALU.subtract)
        for t in range(2):
            nc.scalar.activation(out=d01[:, t, :], in_=diff01[:, t, :], func=ACT.Copy, scale=us_sb[:, t : t + 1])
        for h, cols in enumerate(halves):
            nc.scalar.copy(out=d_bf[h][:, :, 0:2], in_=d01[:, :, cols].rearrange("p e j -> p j e"))
        for t in range(2, PACK):
            for h, cols in enumerate(halves):
                diff = sb.tile([P, HALF], F32, name=f"diff{t}_{h}", align_bytes=64)
                nc.vector.tensor_tensor(
                    diff[:],
                    tea_sb[t][:].indirect(offsets[:, h * HALF // 16 : (h + 1) * HALF // 16]),
                    tanh_z[t][:, cols],
                    ALU.subtract,
                )
                if h == 0:
                    nc.scalar.activation(out=d_bf[h][:, :, t], in_=diff[:], func=ACT.Copy, scale=us_sb[:, t : t + 1])
                else:
                    nc.vector.tensor_scalar(
                        out=d_bf[h][:, :, t], in0=diff[:], scalar1=us_sb[:, t : t + 1], scalar2=None, op0=ALU.mult
                    )
        for h in range(2):
            cols = slice(h * HALF, (h + 1) * HALF)
            nc.vector.quantize_mx(
                out=d_words[:, cols].bitcast(E5M2X4),
                scales=d_plane[:, cols],
                in_=d_bf[h][:].rearrange("p j t -> p (j t)"),
            )

        y = [sb.tile([P, 2, J], F32, name=f"y{u}", align_bytes=64) for u in range(2)]
        out_rows = out_0.rearrange("(p t) j -> t p j", t=PACK)
        for t in range(PACK):
            dx = ps.tile([P, J], F32, name=f"dx{t}")
            nc.tensor.matmul_mx(
                out=dx[:],
                lhsT=wt_dealt[:, 2 * P * t : 2 * P * (t + 1)].bitcast(E2M1X4),
                lhsT_scale=wt_plane_dealt[:, P * t : P * (t + 1)],
                rhs=d_words[:].bitcast(E5M2X4),
                rhs_scale=d_plane[:],
                start=True,
                stop=True,
            )
            pieces = (slice(0, J),) if t < PACK - 1 else halves
            for cols in pieces:
                nc.vector.tensor_tensor(y[t // 2][:, t % 2, cols], res_sb[:, t, cols], dx[:, cols], ALU.subtract)
            nc.sync.dma_start(out=out_rows[t], in_=y[t // 2][:, t % 2, :])

        y_bf = [sb.tile([P, HALF, PACK], BF16, name=f"y_bf{h}", align_bytes=64) for h in range(2)]
        for h, cols in enumerate(halves):
            nc.scalar.copy(out=y_bf[h][:, :, 0:2], in_=y[0][:, :, cols].rearrange("p e j -> p j e"))
        for h, cols in enumerate(halves):
            nc.vector.tensor_copy(out=y_bf[h][:, :, 2:4], in_=y[1][:, :, cols].rearrange("p e j -> p j e"))
        y_words = sb.tile([P, J], U32, name="y_words", align_bytes=64)
        y_plane = sb.tile([P, J], U8, name="y_plane", align_bytes=64)
        out_words = out_1[0].rearrange("p j t -> p (j t)").bitcast(I32)
        for h, cols in enumerate(halves):
            nc.vector.quantize_mx(
                out=y_words[:, cols].bitcast(E4M3X4),
                scales=y_plane[:, cols],
                in_=y_bf[h][:].rearrange("p j t -> p (j t)"),
            )
            nc.sync.dma_start(out=out_words[:, cols], in_=y_words[:, cols].bitcast(I32))
        for r in range(4):
            queue = nc.scalar if r < 2 else nc.sync
            queue.dma_start(out=out_2[0, r:16:4, :].bitcast(I32), in_=y_plane[r:P:32, :].bitcast(I32))
